import numpy as np, ml_dtypes
CORES = [16,32,48,64,80]
N = 5
TOK, K, FT = 256, 2, 1
ROUTE = [[[0,3],[0,1],[3,4],[1,3],[3,4],[0,1],[1,4],[0,3],[2,3],[0,4],[0,1],[2,4],[0,4],[0,3],[1,2],[2,4],[0,4],[0,2],[0,4],[0,2],[0,3],[1,4],[1,4],[2,4],[1,3],[1,2],[1,4],[0,2],[2,4],[0,3],[0,1],[0,3],[0,2],[0,2],[3,4],[3,4],[2,4],[1,2],[2,3],[2,3],[1,3],[0,1],[1,4],[2,4],[2,4],[3,4],[1,3],[3,4],[1,3],[0,2],[0,4],[0,4],[3,4],[0,2],[1,2],[1,3],[0,3],[1,3],[0,4],[2,3],[1,2],[2,4],[3,4],[1,2],[3,4],[0,1],[2,4],[0,4],[0,3],[2,3],[0,3],[1,4],[0,3],[1,2],[0,4],[1,3],[0,1],[2,4],[3,4],[0,3],[3,4],[2,3],[3,4],[1,3],[0,4],[3,4],[1,3],[1,2],[2,3],[3,4],[1,2],[1,3],[2,4],[0,2],[0,4],[1,3],[3,4],[1,2],[1,3],[0,1],[0,3],[0,1],[2,4],[1,4],[0,4],[0,1],[0,4],[0,1],[1,3],[2,4],[0,3],[2,4],[3,4],[2,4],[0,1],[0,2],[0,4],[0,4],[0,3],[2,3],[1,3],[1,4],[0,1],[2,4],[1,4],[1,2],[0,2],[2,3],[1,4],[1,3],[1,4],[1,2],[1,4],[2,3],[2,4],[3,4],[1,2],[2,4],[0,2],[0,2],[2,4],[2,4],[0,1],[0,1],[1,4],[3,4],[2,4],[2,3],[1,2],[0,4],[2,4],[1,4],[0,2],[0,4],[1,2],[0,2],[2,4],[2,3],[0,1],[1,3],[0,2],[3,4],[2,4],[0,2],[0,2],[0,1],[3,4],[0,3],[0,1],[0,4],[1,4],[0,2],[1,3],[1,3],[1,4],[0,3],[0,1],[2,4],[0,1],[1,2],[1,4],[0,2],[3,4],[1,3],[3,4],[1,3],[1,2],[0,2],[0,2],[0,4],[1,4],[1,3],[2,3],[0,3],[3,4],[0,2],[1,4],[0,4],[2,3],[1,2],[1,3],[1,3],[2,4],[2,4],[0,2],[3,4],[2,3],[0,2],[0,1],[0,3],[1,4],[2,3],[0,1],[2,3],[0,2],[1,2],[3,4],[0,1],[1,2],[2,4],[2,3],[0,1],[0,3],[0,1],[0,3],[0,1],[0,1],[0,4],[0,4],[1,3],[2,4],[1,4],[1,3],[0,3],[3,4],[1,4],[0,2],[0,2],[1,4],[2,4],[0,1],[3,4],[3,4],[0,2],[1,2],[0,4],[3,4],[1,2],[3,4],[0,4],[2,3],[0,3],[2,4],[1,4],[3,4],[1,4]],[[1,3],[0,3],[1,3],[0,2],[1,3],[1,3],[0,2],[0,2],[0,4],[0,1],[1,2],[3,4],[0,3],[0,1],[0,1],[0,3],[1,2],[1,2],[2,3],[0,2],[0,3],[0,3],[0,1],[1,4],[1,3],[1,2],[1,4],[2,3],[2,3],[2,3],[0,3],[1,3],[1,3],[2,4],[0,2],[0,3],[0,3],[0,4],[2,3],[2,3],[0,3],[0,4],[1,4],[2,4],[1,3],[1,2],[0,1],[0,3],[1,2],[2,4],[0,4],[1,3],[2,3],[1,4],[0,2],[1,3],[1,2],[3,4],[1,3],[1,4],[0,2],[0,4],[3,4],[1,4],[1,2],[0,1],[0,1],[1,2],[1,4],[0,3],[1,4],[2,3],[1,3],[0,2],[0,1],[0,2],[2,3],[1,3],[0,4],[0,2],[0,4],[2,3],[0,1],[0,4],[1,2],[1,3],[0,3],[0,2],[0,1],[2,4],[1,3],[1,4],[1,3],[2,3],[0,2],[2,3],[0,3],[0,4],[0,4],[0,2],[2,3],[2,3],[0,1],[1,3],[0,4],[1,4],[1,3],[2,3],[2,3],[0,2],[0,4],[0,3],[0,3],[2,4],[0,2],[2,4],[2,3],[0,3],[0,2],[2,3],[1,4],[1,3],[0,2],[2,3],[0,3],[0,3],[0,3],[1,4],[0,1],[3,4],[0,3],[2,4],[0,3],[0,4],[2,3],[1,4],[2,3],[1,4],[3,4],[0,3],[0,1],[1,3],[2,3],[1,2],[2,4],[0,1],[0,2],[3,4],[0,2],[2,3],[0,4],[0,1],[2,4],[2,4],[1,3],[0,1],[0,3],[0,3],[3,4],[0,3],[1,2],[0,1],[2,3],[1,2],[1,3],[1,4],[0,3],[1,4],[1,2],[2,4],[0,4],[1,2],[1,4],[1,4],[0,4],[1,3],[2,3],[2,3],[1,4],[1,2],[3,4],[0,1],[0,1],[0,3],[2,4],[1,2],[1,3],[0,2],[2,4],[2,3],[1,4],[1,2],[0,4],[2,4],[1,3],[2,4],[0,4],[0,4],[3,4],[1,3],[1,2],[1,3],[1,4],[0,2],[0,4],[1,2],[1,3],[1,3],[2,4],[0,3],[0,3],[1,3],[1,3],[0,3],[0,3],[2,4],[0,4],[1,2],[3,4],[0,4],[0,4],[0,1],[1,2],[1,4],[0,4],[1,4],[1,2],[0,4],[0,1],[1,2],[0,4],[1,3],[1,3],[2,4],[1,4],[2,4],[0,2],[0,4],[0,4],[2,3],[0,3],[2,4],[1,4],[0,2],[1,2],[2,3],[2,4],[0,4],[1,4],[0,2],[0,1],[0,4],[2,4],[0,4],[0,4],[1,4]],[[1,4],[2,4],[3,4],[0,3],[0,4],[1,2],[1,3],[0,4],[2,3],[3,4],[3,4],[1,3],[3,4],[0,3],[1,4],[2,4],[2,3],[2,4],[1,4],[1,2],[3,4],[2,4],[1,3],[1,2],[1,3],[3,4],[0,4],[1,3],[0,1],[0,1],[0,1],[1,3],[0,3],[0,3],[1,4],[2,3],[2,3],[2,3],[2,3],[2,3],[0,2],[2,4],[0,2],[1,3],[1,3],[0,1],[0,1],[1,3],[0,3],[1,3],[0,2],[0,4],[2,3],[0,4],[3,4],[0,2],[3,4],[2,3],[0,2],[1,4],[0,4],[3,4],[0,1],[2,3],[1,2],[0,3],[0,4],[0,1],[1,4],[2,4],[1,4],[1,2],[2,4],[3,4],[1,2],[0,4],[2,3],[2,4],[3,4],[0,2],[0,4],[2,3],[3,4],[0,2],[2,3],[0,1],[1,3],[0,4],[1,2],[3,4],[2,4],[1,3],[0,1],[0,2],[3,4],[0,1],[1,4],[1,2],[0,4],[1,2],[0,1],[2,3],[0,1],[1,2],[1,4],[2,4],[0,3],[1,3],[0,3],[3,4],[0,2],[3,4],[0,2],[2,4],[2,4],[1,2],[0,3],[2,3],[1,3],[3,4],[1,2],[0,3],[2,4],[2,3],[0,2],[2,4],[0,3],[0,1],[0,1],[0,1],[1,4],[1,3],[2,3],[2,3],[0,3],[1,3],[2,3],[1,4],[3,4],[1,2],[1,3],[0,2],[3,4],[0,4],[2,4],[1,4],[1,2],[0,3],[0,4],[2,4],[1,2],[2,3],[2,3],[3,4],[2,4],[1,3],[1,3],[1,4],[2,4],[0,1],[2,3],[0,2],[0,4],[0,1],[1,4],[2,3],[3,4],[0,1],[2,3],[2,3],[3,4],[2,4],[3,4],[1,4],[0,2],[1,4],[0,3],[3,4],[3,4],[2,3],[1,2],[0,3],[1,4],[1,4],[1,2],[3,4],[0,4],[1,3],[1,2],[1,4],[1,2],[3,4],[0,2],[0,2],[1,3],[0,4],[3,4],[0,1],[1,4],[1,2],[0,4],[1,4],[1,4],[0,4],[0,2],[3,4],[0,1],[0,3],[0,3],[2,4],[0,1],[1,2],[0,2],[1,4],[0,2],[1,4],[3,4],[3,4],[0,1],[1,3],[3,4],[1,3],[2,3],[0,1],[2,3],[0,2],[1,3],[0,3],[2,4],[3,4],[0,2],[1,3],[1,3],[3,4],[2,4],[2,3],[0,4],[1,3],[0,4],[3,4],[0,3],[1,3],[0,4],[2,4],[0,3],[0,1],[2,3],[0,1],[1,2],[0,1],[0,4],[0,1],[1,4],[2,4],[0,4],[0,4]],[[0,3],[2,3],[0,3],[1,4],[1,4],[0,3],[1,3],[1,2],[0,3],[0,1],[2,3],[0,2],[0,2],[0,4],[1,3],[0,1],[1,2],[2,3],[0,4],[2,3],[0,3],[3,4],[0,4],[0,1],[1,3],[3,4],[3,4],[0,3],[0,2],[0,1],[1,4],[1,4],[2,3],[0,4],[1,2],[2,4],[3,4],[2,4],[0,1],[2,4],[1,4],[1,2],[1,4],[0,4],[0,4],[1,2],[1,4],[1,4],[2,3],[0,2],[0,4],[3,4],[0,2],[0,4],[3,4],[2,4],[0,1],[1,4],[1,2],[2,4],[0,1],[0,3],[0,1],[0,4],[2,4],[0,3],[2,4],[0,3],[0,2],[0,2],[2,3],[0,3],[0,1],[0,3],[1,3],[1,4],[2,3],[2,4],[0,3],[2,3],[0,1],[0,1],[2,4],[0,2],[1,3],[1,3],[1,2],[2,3],[0,3],[2,3],[1,3],[2,4],[0,4],[1,3],[1,2],[0,3],[0,2],[1,2],[0,1],[1,3],[2,3],[0,2],[2,4],[1,3],[1,4],[0,1],[1,4],[0,1],[1,3],[2,4],[0,2],[0,4],[1,3],[0,4],[0,4],[0,3],[3,4],[2,3],[1,4],[0,3],[3,4],[1,3],[0,1],[2,3],[0,1],[0,2],[0,1],[1,2],[2,3],[1,3],[1,4],[0,2],[2,4],[2,4],[0,2],[0,3],[2,4],[2,3],[1,3],[3,4],[3,4],[0,3],[1,2],[1,3],[0,4],[3,4],[0,3],[1,4],[1,2],[0,1],[0,3],[1,2],[1,3],[1,2],[0,2],[2,3],[0,3],[0,1],[0,4],[2,3],[2,4],[0,4],[0,3],[2,4],[2,3],[0,1],[0,1],[1,3],[2,4],[0,3],[0,2],[1,2],[0,2],[2,3],[1,4],[2,3],[1,4],[0,4],[1,2],[0,4],[0,2],[2,3],[1,4],[0,2],[0,2],[3,4],[2,3],[1,2],[2,3],[2,4],[0,4],[0,2],[2,4],[1,2],[0,1],[1,3],[0,4],[1,4],[0,1],[1,2],[3,4],[0,3],[1,4],[1,4],[1,4],[1,4],[0,2],[2,4],[2,4],[2,3],[2,3],[2,4],[2,4],[3,4],[1,3],[2,4],[2,4],[0,3],[2,3],[0,1],[0,1],[1,3],[0,4],[3,4],[0,3],[2,4],[0,1],[0,4],[0,2],[0,4],[1,3],[1,3],[1,3],[0,4],[0,3],[0,3],[1,3],[0,1],[3,4],[3,4],[3,4],[0,1],[1,4],[1,4],[1,2],[1,3],[3,4],[1,4],[1,3],[0,1],[1,2],[2,4],[3,4],[3,4],[1,3],[0,3]],[[0,3],[2,4],[1,4],[0,3],[3,4],[0,4],[3,4],[1,2],[0,1],[0,2],[0,2],[0,1],[0,1],[3,4],[1,4],[3,4],[3,4],[1,4],[0,1],[2,3],[0,2],[1,3],[1,3],[2,4],[2,4],[0,2],[0,2],[1,3],[1,4],[0,1],[0,2],[1,3],[1,4],[0,2],[0,1],[1,2],[1,4],[1,2],[3,4],[1,4],[0,3],[1,4],[1,4],[2,3],[0,1],[3,4],[1,4],[1,4],[0,4],[0,1],[1,2],[0,2],[0,1],[3,4],[0,4],[2,4],[0,1],[2,4],[1,2],[0,4],[0,2],[1,2],[0,2],[2,3],[1,2],[3,4],[2,3],[0,3],[1,2],[2,4],[3,4],[0,4],[1,4],[0,2],[1,3],[1,3],[2,4],[2,3],[1,2],[0,1],[0,2],[2,3],[1,4],[3,4],[0,3],[3,4],[0,4],[1,2],[0,3],[0,1],[1,3],[2,4],[0,1],[0,2],[3,4],[0,2],[1,3],[2,3],[1,3],[0,3],[1,2],[1,2],[2,4],[1,3],[0,1],[2,3],[2,3],[2,4],[2,3],[1,2],[1,4],[3,4],[0,4],[2,3],[1,2],[0,2],[3,4],[0,4],[1,4],[2,4],[1,4],[2,3],[1,2],[2,3],[0,1],[1,3],[0,4],[1,3],[3,4],[0,2],[1,2],[0,4],[1,3],[3,4],[0,4],[0,1],[2,4],[0,4],[2,4],[0,4],[0,1],[1,3],[2,4],[1,3],[0,2],[0,4],[3,4],[1,3],[0,4],[1,4],[0,1],[1,4],[0,3],[0,3],[0,4],[1,4],[2,3],[2,4],[1,3],[2,4],[1,3],[0,1],[3,4],[1,4],[1,4],[1,4],[1,4],[3,4],[3,4],[0,1],[0,3],[1,2],[3,4],[2,4],[0,4],[3,4],[1,3],[1,4],[0,4],[1,4],[1,2],[1,4],[3,4],[0,4],[3,4],[1,4],[1,3],[0,1],[2,4],[0,4],[1,3],[3,4],[1,4],[1,2],[0,1],[1,3],[2,4],[0,4],[0,2],[0,4],[3,4],[3,4],[3,4],[1,4],[0,2],[0,1],[0,3],[1,4],[0,1],[0,1],[0,3],[1,4],[0,3],[2,3],[1,2],[1,4],[1,4],[0,2],[2,4],[0,4],[0,4],[2,4],[2,3],[2,4],[3,4],[2,3],[0,1],[1,3],[2,4],[1,2],[1,3],[1,3],[0,1],[2,3],[0,4],[3,4],[0,3],[3,4],[2,4],[0,4],[0,2],[0,2],[1,3],[2,3],[0,1],[3,4],[2,3],[0,1],[1,3],[1,2],[1,2],[0,1],[2,3],[1,4],[2,4],[1,3]]]
def setup_inputs(rng):
    return {"x": rng.standard_normal((N, 128, TOK), dtype=np.float32).astype(ml_dtypes.bfloat16), "gate": (0.5 * rng.integers(1, 4, size=(N, K, TOK)) * (2 * rng.integers(0, 2, size=(N, K, TOK)) - 1)).astype(np.float32).astype(ml_dtypes.bfloat16), "w1": (rng.standard_normal((N, 128, FT * 128), dtype=np.float32) / 8).astype(ml_dtypes.bfloat16), "w2": (rng.standard_normal((N, 128, FT * 128), dtype=np.float32) / 8).astype(ml_dtypes.bfloat16)}
def setup_inputs_big(rng):
    d = setup_inputs(rng)
    for k in ("x", "gate", "w1", "w2"): d[k] = (d[k].astype(np.float32) * 1024.0).astype(d[k].dtype)
    return d
def setup_inputs_small(rng):
    d = setup_inputs(rng)
    for k in ("x", "gate", "w1", "w2"): d[k] = (d[k].astype(np.float32) * (1 / 1024.0)).astype(d[k].dtype)
    return d
def reference(x, gate, w1, w2):
    X, GATE, W1, W2 = x.astype(np.float64), gate.astype(np.float64), w1.astype(np.float64), w2.astype(np.float64)
    y = np.zeros((N, 128, TOK))
    for r in range(N):
        for t in range(TOK):
            for i, e in enumerate(ROUTE[r][t]):
                hid = np.maximum(W1[e].T @ X[r][:, t], 0.0)
                y[r][:, t] += GATE[r][i, t] * sum(W2[e][:, 128 * f:128 * f + 128].T @ hid[128 * f:128 * f + 128] for f in range(FT))
    return {"y": y.astype(ml_dtypes.bfloat16)}

@@ -1,0 +1,226 @@
+from concourse.mybir import AluOpType
+
+_N, _TOK, _F = 5, 256, 128
+SCRATCH = {
+    "W": ("sbuf", [128, _N * 2 * _F], "bfloat16"),
+    "X": ("sbuf", [128, _TOK], "bfloat16"),
+    "GF": ("sbuf", [128, 2 * _TOK], "bfloat16"),
+    "ONES": ("sbuf", [128, 32], "bfloat16"),
+    "ZERO": ("sbuf", [128, _TOK], "bfloat16"),
+    "TH": ("sbuf", [128, _TOK], "bfloat16"),
+    "R": ("sbuf", [128, 2 * _TOK], "bfloat16"),
+    "D": ("sbuf", [128, 2 * _N * _F], "bfloat16"),
+    "HR": ("sbuf", [128, _N * _TOK], "bfloat16"),
+    "HG": ("sbuf", [128, _N * _TOK], "bfloat16"),
+    "YS": ("sbuf", [128, _TOK], "bfloat16"),
+    "PG": ("psum", [128, 512], "float32"),
+    "GB0": ("psum", [128, 512], "float32"),
+    "GB1": ("psum", [128, 512], "float32"),
+    "GB2": ("psum", [128, 512], "float32"),
+    "PH0": ("psum", [128, 512], "float32"),
+    "PH1": ("psum", [128, 512], "float32"),
+    "PH2": ("psum", [128, 512], "float32"),
+    "PY": ("psum", [128, 512], "float32"),
+}
+SEMAPHORES = (["w", "x", "gt", "one", "zero", "d", "pg", "th", "rr", "loc", "yy", "ys", "out", "gb0", "gb1", "gb2"]
+              + ["wa%d" % i for i in range(_N)] + ["h%d" % i for i in range(_N)]
+              + ["r%d" % i for i in range(_N)] + ["m%d" % i for i in range(_N)])
+
+HELPER_ENGINES = 4
+
+
+def _engine_mask(topo, src, dst, n=None):
+    m = topo.mask(src, dst)
+    e = [i for i in range(m.bit_length()) if (m >> i) & 1]
+    if n is not None and n < len(e):
+        e = e[::len(e) // n][:n]
+    return sum(1 << i for i in e), len(e)
+
+
+def _runs(codes, route_r):
+    c = [codes.index(tuple(p)) for p in route_r]
+    out, t0 = [], 0
+    for t in range(1, len(c) + 1):
+        if t == len(c) or c[t] != c[t0]:
+            out.append((t0, t, c[t0] + 1))
+            t0 = t
+    return out
+
+
+def _helpers(T, topo, home):
+    return [c for c in range(topo.CHIPS * topo.CORES_PER_CHIP)
+            if topo.chip(c) == topo.chip(home) and c != home and T.rank_of(c) is None]
+
+
+def _helper_program(g, core, T, topo, codes, r):
+    home = T.cores[r]
+    hs = _helpers(T, topo, home)
+    j, nh = hs.index(core), len(hs)
+    runs = _runs(codes, T.tables["ROUTE"][r])
+    mine = runs[j * len(runs) // nh:(j + 1) * len(runs) // nh]
+    c0, c1 = mine[0][0], mine[-1][1]
+    v = g.vector
+    v.memset(T.TH[:, c0:c1], 0.0).then_inc(T.sem.d, 1)
+    v.wait_ge(T.sem.d, 1)
+    for (t0, t1, h) in mine:
+        v.memset(T.TH[0:h, t0:t1], 1.0).then_inc(T.sem.d, 1)
+    g.wait_ge(T.sem.d, 1 + len(mine))
+    rid, pid, _ = topo.addr(home)
+    mask, ne = _engine_mask(topo, core, home, HELPER_ENGINES)
+    g.remote_dma(out_ap=T.TH[:, c0:c1], in_ap=T.TH[:, c0:c1], remote_sem=T.sem.th, local_sem=T.sem.loc,
+                 pid=pid, routing_id=rid, dma_engine_mask=mask)
+    g.wait_ge(T.sem.loc, ne)
+
+
+def _decoders(codes, n):
+    blocks = []
+    for e in range(n):
+        for s in range(2):
+            d = [int(codes[k][s] == e) - int(k >= 1 and codes[k - 1][s] == e) for k in range(len(codes))]
+            if any(d):
+                blocks.append((e, s, d))
+    return blocks
+
+
+def _paint(blocks, np_):
+    nb = len(blocks)
+    cur = [[0] * nb for _ in range(np_)]
+    layers = []
+    for k in range(np_ - 1, -1, -1):
+        layer, b = [], 0
+        while b < nb:
+            val = blocks[b][2][k]
+            if cur[k][b] != val:
+                b2 = b + 1
+                while b2 < nb and blocks[b2][2][k] == val and cur[k][b2] != val:
+                    b2 += 1
+                layer.append((k, b, b2, val))
+                for kk in range(k + 1):
+                    for bb in range(b, b2):
+                        cur[kk][bb] = val
+                b = b2
+            else:
+                b += 1
+        if layer:
+            layers.append(layer)
+    return layers
+
+
+def rank_program(g, core, T, topo):
+    route, tok = T.tables["ROUTE"], T.tables["TOK"]
+    cores = list(T.cores)
+    n = len(cores)
+    codes = sorted(set(tuple(p) for r in route for p in r))
+    np_ = len(codes)
+    rank = T.rank_of(core)
+    if rank is None:
+        home = [i for i, c in enumerate(cores) if topo.chip(c) == topo.chip(core)]
+        if home:
+            _helper_program(g, core, T, topo, codes, home[0])
+        return
+
+    S, F = T.sem, _F
+    te, v = g.tensor, g.vector
+    w1 = lambda e: T.W[:, e * 2 * F:e * 2 * F + F]
+    w2 = lambda e: T.W[:, e * 2 * F + F:(e + 1) * 2 * F]
+    order = [rank] + [(rank - s) % n for s in range(1, n)]
+    ph = [T.PH0, T.PH1, T.PH2]
+    gbb = [T.GB0, T.GB1, T.GB2]
+    col = lambda i: slice(i * tok, (i + 1) * tok)
+    gb = lambda i: gbb[i // 2][:, col(i % 2)]
+    gb_full = lambda i: min(2, n - 2 * (i // 2))
+
+    g.sync.dma_start(w1(rank), T.w1[:]).then_inc(S.w, 16)
+    g.scalar.dma_start(w2(rank), T.w2[:]).then_inc(S.w, 16)
+    g.sync.dma_start(T.X[:], T.x[:]).then_inc(S.x, 16)
+    g.scalar.dma_start(T.GF[0:1, 0:2 * tok], T.gate[:]).then_inc(S.gt, 16)
+
+    g.wait_ge(S.w, 32)
+    own = T.W[:, rank * 2 * F:(rank + 1) * 2 * F]
+    sent = 0
+    for s in range(1, n):
+        dst = cores[(rank + s) % n]
+        rid, pid, _ = topo.addr(dst)
+        mask, ne = _engine_mask(topo, core, dst)
+        g.remote_dma(out_ap=own, in_ap=own, remote_sem=S["wa%d" % rank], local_sem=S.loc,
+                     pid=pid, routing_id=rid, dma_engine_mask=mask)
+        sent += ne
+    g.wait_ge(S.loc, sent)
+
+    blocks = _decoders(codes, n)
+    layers = _paint(blocks, np_)
+    v.memset(T.ONES[0:1, 0:np_], 1.0).then_inc(S.one, 1)
+    v.memset(T.ZERO[:], 0.0).then_inc(S.zero, 1)
+    v.memset(T.D[0:np_, 0:len(blocks) * F], 0.0).then_inc(S.d, 1)
+    nd = 1
+    for layer in layers:
+        v.wait_ge(S.d, nd)
+        for (k, b0, b1, val) in layer:
+            v.memset(T.D[0:k + 1, b0 * F:b1 * F], float(val)).then_inc(S.d, 1)
+            nd += 1
+
+    te.wait_ge(S.one, 1)
+    te.wait_ge(S.gt, 16)
+    te.matmul(T.PG[0:np_, 0:2 * tok], lhsT=T.ONES[0:1, 0:np_], rhs=T.GF[0:1, 0:2 * tok],
+              start=True, stop=True).then_inc(S.pg, 1)
+
+    def mm1(i):
+        e = order[i]
+        if i == 0:
+            te.wait_ge(S.w, 32)
+            te.wait_ge(S.x, 16)
+        else:
+            te.wait_ge(S["wa%d" % e], _engine_mask(topo, cores[e], core)[1])
+        if i >= len(ph):
+            te.wait_ge(S["r%d" % (i - len(ph))], 1)
+        te.matmul(ph[i % len(ph)][:, 0:tok], lhsT=w1(e), rhs=T.X[:], start=True, stop=True).then_inc(S["h%d" % i], 1)
+
+    def mm2(i):
+        te.wait_ge(S["m%d" % i], 1)
+        ins = te.matmul(T.PY[:, 0:tok], lhsT=w2(order[i]), rhs=T.HG[:, col(i)], start=(i == 0), stop=(i == n - 1))
+        if i == n - 1:
+            ins.then_inc(S.yy, 1)
+
+    def relu(i):
+        v.wait_ge(S["h%d" % i], 1)
+        v.tensor_tensor(out=T.HR[:, col(i)], in0=ph[i % len(ph)][:, 0:tok], in1=T.ZERO[:],
+                        op=AluOpType.max).then_inc(S["r%d" % i], 1)
+
+    def gatemul(i):
+        v.wait_ge(S["r%d" % i], 1)
+        v.wait_ge(S["gb%d" % (i // 2)], gb_full(i))
+        v.tensor_tensor(out=T.HG[:, col(i)], in0=T.HR[:, col(i)], in1=gb(i),
+                        op=AluOpType.mult).then_inc(S["m%d" % i], 1)
+
+    mm1(0)
+    v.wait_ge(S.zero, 1)
+    relu(0)
+
+    v.wait_ge(S.pg, 1)
+    v.wait_ge(S.th, len(_helpers(T, topo, core)) * HELPER_ENGINES)
+    for s in range(2):
+        v.tensor_tensor(out=T.R[0:np_, col(s)], in0=T.TH[0:np_, 0:tok], in1=T.PG[0:np_, col(s)],
+                        op=AluOpType.mult).then_inc(S.rr, 1)
+    te.wait_ge(S.rr, 2)
+    te.wait_ge(S.d, nd)
+    for i, e in enumerate(order):
+        mine = [(b, blk[1]) for b, blk in enumerate(blocks) if blk[0] == e]
+        for q, (b, s) in enumerate(mine):
+            ins = te.matmul(gb(i), lhsT=T.D[0:np_, b * F:(b + 1) * F], rhs=T.R[0:np_, col(s)],
+                            start=(q == 0), stop=(q == len(mine) - 1))
+        ins.then_inc(S["gb%d" % (i // 2)], 1)
+
+    for i in range(1, n):
+        mm1(i)
+        mm2(i - 1)
+    mm2(n - 1)
+    gatemul(0)
+    for i in range(1, n):
+        relu(i)
+        gatemul(i)
+
+    v.wait_ge(S.yy, 1)
+    v.tensor_copy(out=T.YS[:], in_=T.PY[:, 0:tok]).then_inc(S.ys, 1)
+    g.sync.wait_ge(S.ys, 1)
+    g.sync.dma_start(T.y[:], T.YS[:]).then_inc(S.out, 16)
+    g.sync.wait_ge(S.out, 16)

@@ -5,10 +5,11 @@ SCRATCH = {
     "W": ("sbuf", [128, _N * 2 * _F], "bfloat16"),
     "X": ("sbuf", [128, _TOK], "bfloat16"),
     "GF": ("sbuf", [128, 2 * _TOK], "bfloat16"),
-    "ONES": ("sbuf", [128, 32], "bfloat16"),
+    "ONES": ("sbuf", [128, _F], "bfloat16"),
     "ZERO": ("sbuf", [128, _TOK], "bfloat16"),
     "TH": ("sbuf", [128, _TOK], "bfloat16"),
     "R": ("sbuf", [128, 2 * _TOK], "bfloat16"),
+    "DR": ("sbuf", [128, 512], "bfloat16"),
     "D": ("sbuf", [128, 2 * _N * _F], "bfloat16"),
     "HR": ("sbuf", [128, _N * _TOK], "bfloat16"),
     "HG": ("sbuf", [128, _N * _TOK], "bfloat16"),
@@ -22,11 +23,12 @@ SCRATCH = {
     "PH2": ("psum", [128, 512], "float32"),
     "PY": ("psum", [128, 512], "float32"),
 }
-SEMAPHORES = (["w", "x", "gt", "one", "zero", "d", "pg", "th", "rr", "loc", "yy", "ys", "out", "gb0", "gb1", "gb2"]
+SEMAPHORES = (["w", "x", "gt", "one", "zero", "sd", "d", "pg", "th", "rr", "loc", "yy", "ys", "out"]
+              + ["gb%d" % i for i in range(3)] + ["dp%d" % i for i in range(3)]
               + ["wa%d" % i for i in range(_N)] + ["h%d" % i for i in range(_N)]
               + ["r%d" % i for i in range(_N)] + ["m%d" % i for i in range(_N)])
 
-HELPER_ENGINES = 4
+HELPER_ENGINES = 8
 
 
 def _engine_mask(topo, src, dst, n=None):
@@ -37,14 +39,27 @@ def _engine_mask(topo, src, dst, n=None):
     return sum(1 << i for i in e), len(e)
 
 
-def _runs(codes, route_r):
-    c = [codes.index(tuple(p)) for p in route_r]
-    out, t0 = [], 0
-    for t in range(1, len(c) + 1):
-        if t == len(c) or c[t] != c[t0]:
-            out.append((t0, t, c[t0] + 1))
-            t0 = t
+def _cover(pos):
+    rem, out = set(pos), []
+    while rem:
+        s = sorted(rem)
+        best = (s[0], 1, 1)
+        for i, a in enumerate(s):
+            for b in s[i + 1:]:
+                k = 2
+                while a + k * (b - a) in rem:
+                    k += 1
+                if k > best[2]:
+                    best = (a, b - a, k)
+        out.append(best)
+        for q in range(best[2]):
+            rem.discard(best[0] + q * best[1])
     return out
+
+
+def _cols(ap):
+    a, st, k = ap
+    return slice(a, a + (k - 1) * st + 1, st)
 
 
 def _helpers(T, topo, home):
@@ -56,15 +71,17 @@ def _helper_program(g, core, T, topo, codes, r):
     home = T.cores[r]
     hs = _helpers(T, topo, home)
     j, nh = hs.index(core), len(hs)
-    runs = _runs(codes, T.tables["ROUTE"][r])
-    mine = runs[j * len(runs) // nh:(j + 1) * len(runs) // nh]
-    c0, c1 = mine[0][0], mine[-1][1]
+    code = [codes.index(tuple(p)) for p in T.tables["ROUTE"][r]]
+    c0, c1 = j * len(code) // nh, (j + 1) * len(code) // nh
     v = g.vector
     v.memset(T.TH[:, c0:c1], 0.0).then_inc(T.sem.d, 1)
     v.wait_ge(T.sem.d, 1)
-    for (t0, t1, h) in mine:
-        v.memset(T.TH[0:h, t0:t1], 1.0).then_inc(T.sem.d, 1)
-    g.wait_ge(T.sem.d, 1 + len(mine))
+    nf = 1
+    for p in range(len(codes)):
+        for ap in _cover([t for t in range(c0, c1) if code[t] == p]):
+            v.memset(T.TH[0:p + 1, _cols(ap)], 1.0).then_inc(T.sem.d, 1)
+            nf += 1
+    g.wait_ge(T.sem.d, nf)
     rid, pid, _ = topo.addr(home)
     mask, ne = _engine_mask(topo, core, home, HELPER_ENGINES)
     g.remote_dma(out_ap=T.TH[:, c0:c1], in_ap=T.TH[:, c0:c1], remote_sem=T.sem.th, local_sem=T.sem.loc,
@@ -80,30 +97,6 @@ def _decoders(codes, n):
             if any(d):
                 blocks.append((e, s, d))
     return blocks
-
-
-def _paint(blocks, np_):
-    nb = len(blocks)
-    cur = [[0] * nb for _ in range(np_)]
-    layers = []
-    for k in range(np_ - 1, -1, -1):
-        layer, b = [], 0
-        while b < nb:
-            val = blocks[b][2][k]
-            if cur[k][b] != val:
-                b2 = b + 1
-                while b2 < nb and blocks[b2][2][k] == val and cur[k][b2] != val:
-                    b2 += 1
-                layer.append((k, b, b2, val))
-                for kk in range(k + 1):
-                    for bb in range(b, b2):
-                        cur[kk][bb] = val
-                b = b2
-            else:
-                b += 1
-        if layer:
-            layers.append(layer)
-    return layers
 
 
 def rank_program(g, core, T, topo):
@@ -127,8 +120,9 @@ def rank_program(g, core, T, topo):
     ph = [T.PH0, T.PH1, T.PH2]
     gbb = [T.GB0, T.GB1, T.GB2]
     col = lambda i: slice(i * tok, (i + 1) * tok)
-    gb = lambda i: gbb[i // 2][:, col(i % 2)]
-    gb_full = lambda i: min(2, n - 2 * (i // 2))
+    bank = lambda i: (i + 1) // 2
+    gb = lambda i: gbb[bank(i)][:, col((i + 1) % 2)]
+    gb_full = lambda i: len([q for q in range(n) if bank(q) == bank(i)])
 
     g.sync.dma_start(w1(rank), T.w1[:]).then_inc(S.w, 16)
     g.scalar.dma_start(w2(rank), T.w2[:]).then_inc(S.w, 16)
@@ -148,18 +142,30 @@ def rank_program(g, core, T, topo):
     g.wait_ge(S.loc, sent)
 
     blocks = _decoders(codes, n)
-    layers = _paint(blocks, np_)
-    v.memset(T.ONES[0:1, 0:np_], 1.0).then_inc(S.one, 1)
+    nb = len(blocks)
+    flat = [x for blk in blocks for x in blk[2]]
+    v.memset(T.ONES[0:1, 0:F], 1.0).then_inc(S.one, 1)
+    v.memset(T.DR[0:1, 0:len(flat)], 0.0).then_inc(S.sd, 1)
+    v.wait_ge(S.sd, 1)
+    nsd = 1
+    for val in sorted(set(flat) - {0}):
+        for ap in _cover([i for i, x in enumerate(flat) if x == val]):
+            v.memset(T.DR[0:1, _cols(ap)], float(val)).then_inc(S.sd, 1)
+            nsd += 1
     v.memset(T.ZERO[:], 0.0).then_inc(S.zero, 1)
-    v.memset(T.D[0:np_, 0:len(blocks) * F], 0.0).then_inc(S.d, 1)
-    nd = 1
-    for layer in layers:
-        v.wait_ge(S.d, nd)
-        for (k, b0, b1, val) in layer:
-            v.memset(T.D[0:k + 1, b0 * F:b1 * F], float(val)).then_inc(S.d, 1)
-            nd += 1
-
+    per = 512 // F
     te.wait_ge(S.one, 1)
+    te.wait_ge(S.sd, nsd)
+    for b in range(nb):
+        te.matmul(gbb[b // per][0:np_, (b % per) * F:(b % per + 1) * F], lhsT=T.DR[0:1, b * np_:(b + 1) * np_],
+                  rhs=T.ONES[0:1, 0:F], start=True, stop=True).then_inc(S["dp%d" % (b // per)], 1)
+    ncopy = 0
+    for q in range((nb + per - 1) // per):
+        k = min(per, nb - q * per)
+        v.wait_ge(S["dp%d" % q], k)
+        v.tensor_copy(out=T.D[0:np_, q * 512:q * 512 + k * F], in_=gbb[q][0:np_, 0:k * F]).then_inc(S.d, 1)
+        ncopy += 1
+
     te.wait_ge(S.gt, 16)
     te.matmul(T.PG[0:np_, 0:2 * tok], lhsT=T.ONES[0:1, 0:np_], rhs=T.GF[0:1, 0:2 * tok],
               start=True, stop=True).then_inc(S.pg, 1)
@@ -188,7 +194,7 @@ def rank_program(g, core, T, topo):
 
     def gatemul(i):
         v.wait_ge(S["r%d" % i], 1)
-        v.wait_ge(S["gb%d" % (i // 2)], gb_full(i))
+        v.wait_ge(S["gb%d" % bank(i)], gb_full(i))
         v.tensor_tensor(out=T.HG[:, col(i)], in0=T.HR[:, col(i)], in1=gb(i),
                         op=AluOpType.mult).then_inc(S["m%d" % i], 1)
 
@@ -202,13 +208,13 @@ def rank_program(g, core, T, topo):
         v.tensor_tensor(out=T.R[0:np_, col(s)], in0=T.TH[0:np_, 0:tok], in1=T.PG[0:np_, col(s)],
                         op=AluOpType.mult).then_inc(S.rr, 1)
     te.wait_ge(S.rr, 2)
-    te.wait_ge(S.d, nd)
+    te.wait_ge(S.d, ncopy)
     for i, e in enumerate(order):
         mine = [(b, blk[1]) for b, blk in enumerate(blocks) if blk[0] == e]
         for q, (b, s) in enumerate(mine):
             ins = te.matmul(gb(i), lhsT=T.D[0:np_, b * F:(b + 1) * F], rhs=T.R[0:np_, col(s)],
                             start=(q == 0), stop=(q == len(mine) - 1))
-        ins.then_inc(S["gb%d" % (i // 2)], 1)
+        ins.then_inc(S["gb%d" % bank(i)], 1)
 
     for i in range(1, n):
         mm1(i)

@@ -1,4 +1,5 @@
-from concourse.mybir import AluOpType
+from concourse.bass import DstId, RemoteDMATransfer
+from concourse.mybir import AluOpType, ActivationFunctionType
 
 _N, _TOK, _F = 5, 256, 128
 SCRATCH = {
@@ -6,11 +7,10 @@ SCRATCH = {
     "X": ("sbuf", [128, _TOK], "bfloat16"),
     "GF": ("sbuf", [128, 2 * _TOK], "bfloat16"),
     "ONES": ("sbuf", [128, _F], "bfloat16"),
-    "ZERO": ("sbuf", [128, _TOK], "bfloat16"),
     "TH": ("sbuf", [128, _TOK], "bfloat16"),
-    "R": ("sbuf", [128, 2 * _TOK], "bfloat16"),
+    "R": ("sbuf", [128, _TOK], "bfloat16"),
     "DR": ("sbuf", [128, 512], "bfloat16"),
-    "D": ("sbuf", [128, 2 * _N * _F], "bfloat16"),
+    "D": ("sbuf", [128, _N * _F], "bfloat16"),
     "HR": ("sbuf", [128, _N * _TOK], "bfloat16"),
     "HG": ("sbuf", [128, _N * _TOK], "bfloat16"),
     "YS": ("sbuf", [128, _TOK], "bfloat16"),
@@ -23,12 +23,14 @@ SCRATCH = {
     "PH2": ("psum", [128, 512], "float32"),
     "PY": ("psum", [128, 512], "float32"),
 }
-SEMAPHORES = (["w", "x", "gt", "one", "zero", "sd", "d", "pg", "th", "rr", "loc", "yy", "ys", "out"]
-              + ["gb%d" % i for i in range(3)] + ["dp%d" % i for i in range(3)]
-              + ["wa%d" % i for i in range(_N)] + ["h%d" % i for i in range(_N)]
+SEMAPHORES = (["w", "x", "gt", "one", "sd", "d", "pg", "th", "rr", "loc", "yya", "yyb", "ys", "out", "dp0", "dp1"]
+              + ["gb%d" % i for i in range(3)]
+              + ["wa%d" % i for i in range(_N)] + ["wb%d" % i for i in range(_N)] + ["h%d" % i for i in range(_N)]
               + ["r%d" % i for i in range(_N)] + ["m%d" % i for i in range(_N)])
 
 HELPER_ENGINES = 8
+PLAN = [((1, 2), "w"), ((3, 4), "w1"), ((3, 4), "w2")]
+TORDER = [("a", 1), ("a", 2), ("a", 3), ("a", 4), ("b", 1), ("b", 2), ("b", 3), ("b", 4)]
 
 
 def _engine_mask(topo, src, dst, n=None):
@@ -79,7 +81,7 @@ def _helper_program(g, core, T, topo, codes, r):
     nf = 1
     for p in range(len(codes)):
         for ap in _cover([t for t in range(c0, c1) if code[t] == p]):
-            v.memset(T.TH[0:p + 1, _cols(ap)], 1.0).then_inc(T.sem.d, 1)
+            v.memset(T.TH[0:2 * (p + 1), _cols(ap)], 1.0).then_inc(T.sem.d, 1)
             nf += 1
     g.wait_ge(T.sem.d, nf)
     rid, pid, _ = topo.addr(home)
@@ -90,13 +92,8 @@ def _helper_program(g, core, T, topo, codes, r):
 
 
 def _decoders(codes, n):
-    blocks = []
-    for e in range(n):
-        for s in range(2):
-            d = [int(codes[k][s] == e) - int(k >= 1 and codes[k - 1][s] == e) for k in range(len(codes))]
-            if any(d):
-                blocks.append((e, s, d))
-    return blocks
+    return [[int(codes[k][s] == e) - int(k >= 1 and codes[k - 1][s] == e)
+             for k in range(len(codes)) for s in range(2)] for e in range(n)]
 
 
 def rank_program(g, core, T, topo):
@@ -104,7 +101,7 @@ def rank_program(g, core, T, topo):
     cores = list(T.cores)
     n = len(cores)
     codes = sorted(set(tuple(p) for r in route for p in r))
-    np_ = len(codes)
+    k2 = 2 * len(codes)
     rank = T.rank_of(core)
     if rank is None:
         home = [i for i, c in enumerate(cores) if topo.chip(c) == topo.chip(core)]
@@ -113,7 +110,7 @@ def rank_program(g, core, T, topo):
         return
 
     S, F = T.sem, _F
-    te, v = g.tensor, g.vector
+    te, v, sc = g.tensor, g.vector, g.scalar
     w1 = lambda e: T.W[:, e * 2 * F:e * 2 * F + F]
     w2 = lambda e: T.W[:, e * 2 * F + F:(e + 1) * 2 * F]
     order = [rank] + [(rank - s) % n for s in range(1, n)]
@@ -125,25 +122,35 @@ def rank_program(g, core, T, topo):
     gb_full = lambda i: len([q for q in range(n) if bank(q) == bank(i)])
 
     g.sync.dma_start(w1(rank), T.w1[:]).then_inc(S.w, 16)
-    g.scalar.dma_start(w2(rank), T.w2[:]).then_inc(S.w, 16)
+    sc.dma_start(w2(rank), T.w2[:]).then_inc(S.w, 16)
     g.sync.dma_start(T.X[:], T.x[:]).then_inc(S.x, 16)
-    g.scalar.dma_start(T.GF[0:1, 0:2 * tok], T.gate[:]).then_inc(S.gt, 16)
+    sc.dma_start(T.GF[0:1, 0:2 * tok], T.gate[:]).then_inc(S.gt, 16)
 
     g.wait_ge(S.w, 32)
-    own = T.W[:, rank * 2 * F:(rank + 1) * 2 * F]
+    part = {"w": (T.W[:, rank * 2 * F:(rank + 1) * 2 * F], S["wa%d" % rank]),
+            "w1": (w1(rank), S["wa%d" % rank]), "w2": (w2(rank), S["wb%d" % rank])}
+    cut = [s for steps, p in PLAN if p == "w2" for s in steps]
     sent = 0
-    for s in range(1, n):
-        dst = cores[(rank + s) % n]
-        rid, pid, _ = topo.addr(dst)
-        mask, ne = _engine_mask(topo, core, dst)
-        g.remote_dma(out_ap=own, in_ap=own, remote_sem=S["wa%d" % rank], local_sem=S.loc,
-                     pid=pid, routing_id=rid, dma_engine_mask=mask)
+    for steps, p in PLAN:
+        ap, sem = part[p]
+        dsts = [cores[(rank + s) % n] for s in steps]
+        mask, ne = _engine_mask(topo, core, dsts[0])
+        for d in dsts:
+            mask &= _engine_mask(topo, core, d)[0]
+        if len(dsts) == 1:
+            rid, pid, _ = topo.addr(dsts[0])
+            g.remote_dma(out_ap=ap, in_ap=ap, remote_sem=sem, local_sem=S.loc, pid=pid, routing_id=rid,
+                         dma_engine_mask=mask)
+        else:
+            ids = [DstId(rid=topo.addr(d)[0], pnc=topo.addr(d)[1]) for d in dsts]
+            g.remote_dma_fused([RemoteDMATransfer(dst_ids=ids, dma_engine_mask=mask, remote_sem=sem,
+                                                  srcs=[ap], dsts=[ap for _ in dsts])], local_sem=S.loc)
         sent += ne
     g.wait_ge(S.loc, sent)
 
     blocks = _decoders(codes, n)
-    nb = len(blocks)
-    flat = [x for blk in blocks for x in blk[2]]
+    alt = n * k2
+    flat = [x for d in blocks for x in d] + [int(j % 2 == s) for s in range(2) for j in range(k2)]
     v.memset(T.ONES[0:1, 0:F], 1.0).then_inc(S.one, 1)
     v.memset(T.DR[0:1, 0:len(flat)], 0.0).then_inc(S.sd, 1)
     v.wait_ge(S.sd, 1)
@@ -152,23 +159,25 @@ def rank_program(g, core, T, topo):
         for ap in _cover([i for i, x in enumerate(flat) if x == val]):
             v.memset(T.DR[0:1, _cols(ap)], float(val)).then_inc(S.sd, 1)
             nsd += 1
-    v.memset(T.ZERO[:], 0.0).then_inc(S.zero, 1)
-    per = 512 // F
+    per = (n + 1) // 2
     te.wait_ge(S.one, 1)
     te.wait_ge(S.sd, nsd)
-    for b in range(nb):
-        te.matmul(gbb[b // per][0:np_, (b % per) * F:(b % per + 1) * F], lhsT=T.DR[0:1, b * np_:(b + 1) * np_],
-                  rhs=T.ONES[0:1, 0:F], start=True, stop=True).then_inc(S["dp%d" % (b // per)], 1)
-    ncopy = 0
-    for q in range((nb + per - 1) // per):
-        k = min(per, nb - q * per)
-        v.wait_ge(S["dp%d" % q], k)
-        v.tensor_copy(out=T.D[0:np_, q * 512:q * 512 + k * F], in_=gbb[q][0:np_, 0:k * F]).then_inc(S.d, 1)
-        ncopy += 1
+    for b in range(n):
+        q, o = (0, b) if b < per else (1, b - per)
+        te.matmul(gbb[q][0:k2, o * F:(o + 1) * F], lhsT=T.DR[0:1, b * k2:(b + 1) * k2],
+                  rhs=T.ONES[0:1, 0:F], start=True, stop=True).then_inc(S["dp%d" % q], 1)
+    v.wait_ge(S.dp0, per)
+    v.tensor_copy(out=T.D[0:k2, 0:per * F], in_=gbb[0][0:k2, 0:per * F]).then_inc(S.d, 1)
+    sc.wait_ge(S.dp1, n - per)
+    sc.activation(out=T.D[0:k2, per * F:n * F], in_=gbb[1][0:k2, 0:(n - per) * F],
+                  func=ActivationFunctionType.Copy).then_inc(S.d, 1)
 
     te.wait_ge(S.gt, 16)
-    te.matmul(T.PG[0:np_, 0:2 * tok], lhsT=T.ONES[0:1, 0:np_], rhs=T.GF[0:1, 0:2 * tok],
-              start=True, stop=True).then_inc(S.pg, 1)
+    te.matmul(T.PG[0:k2, 0:tok], lhsT=T.DR[0:1, alt:alt + k2], rhs=T.GF[0:1, 0:tok], start=True, stop=False)
+    te.matmul(T.PG[0:k2, 0:tok], lhsT=T.DR[0:1, alt + k2:alt + 2 * k2], rhs=T.GF[0:1, tok:2 * tok],
+              start=False, stop=True).then_inc(S.pg, 1)
+
+    arrive = lambda e: _engine_mask(topo, cores[e], core)[1]
 
     def mm1(i):
         e = order[i]
@@ -176,21 +185,34 @@ def rank_program(g, core, T, topo):
             te.wait_ge(S.w, 32)
             te.wait_ge(S.x, 16)
         else:
-            te.wait_ge(S["wa%d" % e], _engine_mask(topo, cores[e], core)[1])
+            te.wait_ge(S["wa%d" % e], arrive(e))
         if i >= len(ph):
             te.wait_ge(S["r%d" % (i - len(ph))], 1)
         te.matmul(ph[i % len(ph)][:, 0:tok], lhsT=w1(e), rhs=T.X[:], start=True, stop=True).then_inc(S["h%d" % i], 1)
 
+    half = tok // 2
+    ybank = [(T.PY, S.yya), (T.PG, S.yyb)]
+
     def mm2(i):
+        e = order[i]
         te.wait_ge(S["m%d" % i], 1)
-        ins = te.matmul(T.PY[:, 0:tok], lhsT=w2(order[i]), rhs=T.HG[:, col(i)], start=(i == 0), stop=(i == n - 1))
-        if i == n - 1:
-            ins.then_inc(S.yy, 1)
+        if i in cut:
+            te.wait_ge(S["wb%d" % e], arrive(e))
+        for hf, (pb, sem) in enumerate(ybank):
+            ins = te.matmul(pb[:, 0:half], lhsT=w2(e), rhs=T.HG[:, i * tok + hf * half:i * tok + (hf + 1) * half],
+                            start=(i == 0), stop=(i == n - 1))
+            if i == n - 1:
+                ins.then_inc(sem, 1)
+
+    def gates(i):
+        e = order[i]
+        te.matmul(gb(i), lhsT=T.D[0:k2, e * F:(e + 1) * F], rhs=T.R[0:k2, 0:tok],
+                  start=True, stop=True).then_inc(S["gb%d" % bank(i)], 1)
 
     def relu(i):
-        v.wait_ge(S["h%d" % i], 1)
-        v.tensor_tensor(out=T.HR[:, col(i)], in0=ph[i % len(ph)][:, 0:tok], in1=T.ZERO[:],
-                        op=AluOpType.max).then_inc(S["r%d" % i], 1)
+        sc.wait_ge(S["h%d" % i], 1)
+        sc.activation(out=T.HR[:, col(i)], in_=ph[i % len(ph)][:, 0:tok],
+                      func=ActivationFunctionType.Relu).then_inc(S["r%d" % i], 1)
 
     def gatemul(i):
         v.wait_ge(S["r%d" % i], 1)
@@ -198,35 +220,30 @@ def rank_program(g, core, T, topo):
         v.tensor_tensor(out=T.HG[:, col(i)], in0=T.HR[:, col(i)], in1=gb(i),
                         op=AluOpType.mult).then_inc(S["m%d" % i], 1)
 
-    mm1(0)
-    v.wait_ge(S.zero, 1)
-    relu(0)
-
     v.wait_ge(S.pg, 1)
     v.wait_ge(S.th, len(_helpers(T, topo, core)) * HELPER_ENGINES)
-    for s in range(2):
-        v.tensor_tensor(out=T.R[0:np_, col(s)], in0=T.TH[0:np_, 0:tok], in1=T.PG[0:np_, col(s)],
-                        op=AluOpType.mult).then_inc(S.rr, 1)
-    te.wait_ge(S.rr, 2)
-    te.wait_ge(S.d, ncopy)
-    for i, e in enumerate(order):
-        mine = [(b, blk[1]) for b, blk in enumerate(blocks) if blk[0] == e]
-        for q, (b, s) in enumerate(mine):
-            ins = te.matmul(gb(i), lhsT=T.D[0:np_, b * F:(b + 1) * F], rhs=T.R[0:np_, col(s)],
-                            start=(q == 0), stop=(q == len(mine) - 1))
-        ins.then_inc(S["gb%d" % bank(i)], 1)
+    v.tensor_tensor(out=T.R[0:k2, 0:tok], in0=T.TH[0:k2, 0:tok], in1=T.PG[0:k2, 0:tok],
+                    op=AluOpType.mult).then_inc(S.rr, 1)
 
-    for i in range(1, n):
-        mm1(i)
-        mm2(i - 1)
-    mm2(n - 1)
-    gatemul(0)
-    for i in range(1, n):
+    mm1(0)
+    te.wait_ge(S.rr, 1)
+    te.wait_ge(S.d, 2)
+    gates(0)
+    gates(1)
+    gates(2)
+    mm2(0)
+    gates(3)
+    gates(4)
+    for kind, i in TORDER:
+        (mm1 if kind == "a" else mm2)(i)
+    for i in range(n):
         relu(i)
         gatemul(i)
 
-    v.wait_ge(S.yy, 1)
-    v.tensor_copy(out=T.YS[:], in_=T.PY[:, 0:tok]).then_inc(S.ys, 1)
-    g.sync.wait_ge(S.ys, 1)
+    v.wait_ge(S.yya, 1)
+    v.tensor_copy(out=T.YS[:, 0:half], in_=T.PY[:, 0:half]).then_inc(S.ys, 1)
+    sc.wait_ge(S.yyb, 1)
+    sc.activation(out=T.YS[:, half:tok], in_=T.PG[:, 0:half], func=ActivationFunctionType.Copy).then_inc(S.ys, 1)
+    g.sync.wait_ge(S.ys, 2)
     g.sync.dma_start(T.y[:], T.YS[:]).then_inc(S.out, 16)
     g.sync.wait_ge(S.out, 16)

from concourse.bass import DstId, RemoteDMATransfer
from concourse.mybir import AluOpType, ActivationFunctionType

_N, _TOK, _F = 5, 256, 128
SCRATCH = {
    "W": ("sbuf", [128, _N * 2 * _F], "bfloat16"),
    "X": ("sbuf", [128, _TOK], "bfloat16"),
    "GF": ("sbuf", [128, 2 * _TOK], "bfloat16"),
    "ONES": ("sbuf", [128, _F], "bfloat16"),
    "TH": ("sbuf", [128, _TOK], "bfloat16"),
    "R": ("sbuf", [128, _TOK], "bfloat16"),
    "DR": ("sbuf", [128, 512], "bfloat16"),
    "D": ("sbuf", [128, _N * _F], "bfloat16"),
    "HR": ("sbuf", [128, _N * _TOK], "bfloat16"),
    "HG": ("sbuf", [128, _N * _TOK], "bfloat16"),
    "YS": ("sbuf", [128, _TOK], "bfloat16"),
    "PG": ("psum", [128, 512], "float32"),
    "GB0": ("psum", [128, 512], "float32"),
    "GB1": ("psum", [128, 512], "float32"),
    "GB2": ("psum", [128, 512], "float32"),
    "PH0": ("psum", [128, 512], "float32"),
    "PH1": ("psum", [128, 512], "float32"),
    "PH2": ("psum", [128, 512], "float32"),
    "PY": ("psum", [128, 512], "float32"),
}
SEMAPHORES = (["w", "x", "gt", "one", "sd", "d", "pg", "th", "rr", "loc", "yya", "yyb", "ys", "out", "dp0", "dp1"]
              + ["gb%d" % i for i in range(3)]
              + ["wa%d" % i for i in range(_N)] + ["wb%d" % i for i in range(_N)] + ["h%d" % i for i in range(_N)]
              + ["r%d" % i for i in range(_N)] + ["m%d" % i for i in range(_N)])

HELPER_ENGINES = 8
PLAN = [((1, 2), "w"), ((3, 4), "w1"), ((3, 4), "w2")]
TORDER = [("a", 1), ("a", 2), ("a", 3), ("a", 4), ("b", 1), ("b", 2), ("b", 3), ("b", 4)]


def _engine_mask(topo, src, dst, n=None):
    m = topo.mask(src, dst)
    e = [i for i in range(m.bit_length()) if (m >> i) & 1]
    if n is not None and n < len(e):
        e = e[::len(e) // n][:n]
    return sum(1 << i for i in e), len(e)


def _cover(pos):
    rem, out = set(pos), []
    while rem:
        s = sorted(rem)
        best = (s[0], 1, 1)
        for i, a in enumerate(s):
            for b in s[i + 1:]:
                k = 2
                while a + k * (b - a) in rem:
                    k += 1
                if k > best[2]:
                    best = (a, b - a, k)
        out.append(best)
        for q in range(best[2]):
            rem.discard(best[0] + q * best[1])
    return out


def _cols(ap):
    a, st, k = ap
    return slice(a, a + (k - 1) * st + 1, st)


def _helpers(T, topo, home):
    return [c for c in range(topo.CHIPS * topo.CORES_PER_CHIP)
            if topo.chip(c) == topo.chip(home) and c != home and T.rank_of(c) is None]


def _helper_program(g, core, T, topo, codes, r):
    home = T.cores[r]
    hs = _helpers(T, topo, home)
    j, nh = hs.index(core), len(hs)
    code = [codes.index(tuple(p)) for p in T.tables["ROUTE"][r]]
    c0, c1 = j * len(code) // nh, (j + 1) * len(code) // nh
    v = g.vector
    v.memset(T.TH[:, c0:c1], 0.0).then_inc(T.sem.d, 1)
    v.wait_ge(T.sem.d, 1)
    nf = 1
    for p in range(len(codes)):
        for ap in _cover([t for t in range(c0, c1) if code[t] == p]):
            v.memset(T.TH[0:2 * (p + 1), _cols(ap)], 1.0).then_inc(T.sem.d, 1)
            nf += 1
    g.wait_ge(T.sem.d, nf)
    rid, pid, _ = topo.addr(home)
    mask, ne = _engine_mask(topo, core, home, HELPER_ENGINES)
    g.remote_dma(out_ap=T.TH[:, c0:c1], in_ap=T.TH[:, c0:c1], remote_sem=T.sem.th, local_sem=T.sem.loc,
                 pid=pid, routing_id=rid, dma_engine_mask=mask)
    g.wait_ge(T.sem.loc, ne)


def _decoders(codes, n):
    return [[int(codes[k][s] == e) - int(k >= 1 and codes[k - 1][s] == e)
             for k in range(len(codes)) for s in range(2)] for e in range(n)]


def rank_program(g, core, T, topo):
    route, tok = T.tables["ROUTE"], T.tables["TOK"]
    cores = list(T.cores)
    n = len(cores)
    codes = sorted(set(tuple(p) for r in route for p in r))
    k2 = 2 * len(codes)
    rank = T.rank_of(core)
    if rank is None:
        home = [i for i, c in enumerate(cores) if topo.chip(c) == topo.chip(core)]
        if home:
            _helper_program(g, core, T, topo, codes, home[0])
        return

    S, F = T.sem, _F
    te, v, sc = g.tensor, g.vector, g.scalar
    w1 = lambda e: T.W[:, e * 2 * F:e * 2 * F + F]
    w2 = lambda e: T.W[:, e * 2 * F + F:(e + 1) * 2 * F]
    order = [rank] + [(rank - s) % n for s in range(1, n)]
    ph = [T.PH0, T.PH1, T.PH2]
    gbb = [T.GB0, T.GB1, T.GB2]
    col = lambda i: slice(i * tok, (i + 1) * tok)
    bank = lambda i: (i + 1) // 2
    gb = lambda i: gbb[bank(i)][:, col((i + 1) % 2)]
    gb_full = lambda i: len([q for q in range(n) if bank(q) == bank(i)])

    g.sync.dma_start(w1(rank), T.w1[:]).then_inc(S.w, 16)
    sc.dma_start(w2(rank), T.w2[:]).then_inc(S.w, 16)
    g.sync.dma_start(T.X[:], T.x[:]).then_inc(S.x, 16)
    sc.dma_start(T.GF[0:1, 0:2 * tok], T.gate[:]).then_inc(S.gt, 16)

    g.wait_ge(S.w, 32)
    part = {"w": (T.W[:, rank * 2 * F:(rank + 1) * 2 * F], S["wa%d" % rank]),
            "w1": (w1(rank), S["wa%d" % rank]), "w2": (w2(rank), S["wb%d" % rank])}
    cut = [s for steps, p in PLAN if p == "w2" for s in steps]
    sent = 0
    for steps, p in PLAN:
        ap, sem = part[p]
        dsts = [cores[(rank + s) % n] for s in steps]
        mask, ne = _engine_mask(topo, core, dsts[0])
        for d in dsts:
            mask &= _engine_mask(topo, core, d)[0]
        if len(dsts) == 1:
            rid, pid, _ = topo.addr(dsts[0])
            g.remote_dma(out_ap=ap, in_ap=ap, remote_sem=sem, local_sem=S.loc, pid=pid, routing_id=rid,
                         dma_engine_mask=mask)
        else:
            ids = [DstId(rid=topo.addr(d)[0], pnc=topo.addr(d)[1]) for d in dsts]
            g.remote_dma_fused([RemoteDMATransfer(dst_ids=ids, dma_engine_mask=mask, remote_sem=sem,
                                                  srcs=[ap], dsts=[ap for _ in dsts])], local_sem=S.loc)
        sent += ne
    g.wait_ge(S.loc, sent)

    blocks = _decoders(codes, n)
    alt = n * k2
    flat = [x for d in blocks for x in d] + [int(j % 2 == s) for s in range(2) for j in range(k2)]
    v.memset(T.ONES[0:1, 0:F], 1.0).then_inc(S.one, 1)
    v.memset(T.DR[0:1, 0:len(flat)], 0.0).then_inc(S.sd, 1)
    v.wait_ge(S.sd, 1)
    nsd = 1
    for val in sorted(set(flat) - {0}):
        for ap in _cover([i for i, x in enumerate(flat) if x == val]):
            v.memset(T.DR[0:1, _cols(ap)], float(val)).then_inc(S.sd, 1)
            nsd += 1
    per = (n + 1) // 2
    te.wait_ge(S.one, 1)
    te.wait_ge(S.sd, nsd)
    for b in range(n):
        q, o = (0, b) if b < per else (1, b - per)
        te.matmul(gbb[q][0:k2, o * F:(o + 1) * F], lhsT=T.DR[0:1, b * k2:(b + 1) * k2],
                  rhs=T.ONES[0:1, 0:F], start=True, stop=True).then_inc(S["dp%d" % q], 1)
    v.wait_ge(S.dp0, per)
    v.tensor_copy(out=T.D[0:k2, 0:per * F], in_=gbb[0][0:k2, 0:per * F]).then_inc(S.d, 1)
    sc.wait_ge(S.dp1, n - per)
    sc.activation(out=T.D[0:k2, per * F:n * F], in_=gbb[1][0:k2, 0:(n - per) * F],
                  func=ActivationFunctionType.Copy).then_inc(S.d, 1)

    te.wait_ge(S.gt, 16)
    te.matmul(T.PG[0:k2, 0:tok], lhsT=T.DR[0:1, alt:alt + k2], rhs=T.GF[0:1, 0:tok], start=True, stop=False)
    te.matmul(T.PG[0:k2, 0:tok], lhsT=T.DR[0:1, alt + k2:alt + 2 * k2], rhs=T.GF[0:1, tok:2 * tok],
              start=False, stop=True).then_inc(S.pg, 1)

    arrive = lambda e: _engine_mask(topo, cores[e], core)[1]

    def mm1(i):
        e = order[i]
        if i == 0:
            te.wait_ge(S.w, 32)
            te.wait_ge(S.x, 16)
        else:
            te.wait_ge(S["wa%d" % e], arrive(e))
        if i >= len(ph):
            te.wait_ge(S["r%d" % (i - len(ph))], 1)
        te.matmul(ph[i % len(ph)][:, 0:tok], lhsT=w1(e), rhs=T.X[:], start=True, stop=True).then_inc(S["h%d" % i], 1)

    half = tok // 2
    ybank = [(T.PY, S.yya), (T.PG, S.yyb)]

    def mm2(i):
        e = order[i]
        te.wait_ge(S["m%d" % i], 1)
        if i in cut:
            te.wait_ge(S["wb%d" % e], arrive(e))
        for hf, (pb, sem) in enumerate(ybank):
            ins = te.matmul(pb[:, 0:half], lhsT=w2(e), rhs=T.HG[:, i * tok + hf * half:i * tok + (hf + 1) * half],
                            start=(i == 0), stop=(i == n - 1))
            if i == n - 1:
                ins.then_inc(sem, 1)

    def gates(i):
        e = order[i]
        te.matmul(gb(i), lhsT=T.D[0:k2, e * F:(e + 1) * F], rhs=T.R[0:k2, 0:tok],
                  start=True, stop=True).then_inc(S["gb%d" % bank(i)], 1)

    def relu(i):
        sc.wait_ge(S["h%d" % i], 1)
        sc.activation(out=T.HR[:, col(i)], in_=ph[i % len(ph)][:, 0:tok],
                      func=ActivationFunctionType.Relu).then_inc(S["r%d" % i], 1)

    def gatemul(i):
        v.wait_ge(S["r%d" % i], 1)
        v.wait_ge(S["gb%d" % bank(i)], gb_full(i))
        v.tensor_tensor(out=T.HG[:, col(i)], in0=T.HR[:, col(i)], in1=gb(i),
                        op=AluOpType.mult).then_inc(S["m%d" % i], 1)

    v.wait_ge(S.pg, 1)
    v.wait_ge(S.th, len(_helpers(T, topo, core)) * HELPER_ENGINES)
    v.tensor_tensor(out=T.R[0:k2, 0:tok], in0=T.TH[0:k2, 0:tok], in1=T.PG[0:k2, 0:tok],
                    op=AluOpType.mult).then_inc(S.rr, 1)

    mm1(0)
    te.wait_ge(S.rr, 1)
    te.wait_ge(S.d, 2)
    gates(0)
    gates(1)
    gates(2)
    mm2(0)
    gates(3)
    gates(4)
    for kind, i in TORDER:
        (mm1 if kind == "a" else mm2)(i)
    for i in range(n):
        relu(i)
        gatemul(i)

    v.wait_ge(S.yya, 1)
    v.tensor_copy(out=T.YS[:, 0:half], in_=T.PY[:, 0:half]).then_inc(S.ys, 1)
    sc.wait_ge(S.yyb, 1)
    sc.activation(out=T.YS[:, half:tok], in_=T.PG[:, 0:half], func=ActivationFunctionType.Copy).then_inc(S.ys, 1)
    g.sync.wait_ge(S.ys, 2)
    g.sync.dma_start(T.y[:], T.YS[:]).then_inc(S.out, 16)
    g.sync.wait_ge(S.out, 16)
